import numpy as np, ml_dtypes
CORES = [40,64,80,88,96,104,120,144]
N = 8
BF = ml_dtypes.bfloat16
V, G, ST, RO = 1008, 960, 7, 3
D, B, Q = 48, 240, 48
C, W = 144, 1968
def pack(xx, yy, nl, al):
    h = lambda a: np.ascontiguousarray(a).reshape(N, 128, V)
    return {"xf": h(xx).astype(np.float32).astype(BF), "lab": h(yy).astype(np.float32).astype(BF), "nb": h(nl).astype(np.int32), "asc": h(al).astype(np.int32)}
def signs(rng, *shape):
    return rng.integers(0, 2, shape) * 2 - 1
def both(c):
    return np.concatenate([c, np.roll(c, -1, axis=0)[..., :G]], axis=-1)
def alike(rng, c, want):
    o = np.argsort(c, axis=2, kind="stable"); n = np.sum(c < 0, axis=2)[:, :, None]; m = c.shape[2]
    j = np.where(want < 0, rng.random(want.shape) * n, n + rng.random(want.shape) * (m - n)).astype(np.int64)
    return np.take_along_axis(o, np.minimum(j, m - 1), 2)
def parts(rng):
    pat = signs(rng, 1, 8, 16, 1); c = signs(rng, N, 8, V)
    yy = c[:, :, None, :] * pat; yy = np.where(rng.random(yy.shape) < 0.1, -yy, yy)
    xx = rng.integers(0, 16, (N, 8, 16, V)); nl = rng.integers(0, W, (N, 8, 16, V))
    al = alike(rng, c, np.repeat(c[:, :, None, :], 16, axis=2).reshape(N, 8, 16 * V)).reshape(N, 8, 16, V)
    al = np.where(rng.random(al.shape) < 0.1, rng.integers(0, V, al.shape), al)
    r, g, i, v = np.indices((N, 8, 4, V))
    nl[r, g, rng.integers(1, 16, r.shape), al[:, :, :4]] = v
    share = rng.choice(np.array([0.1, 0.4, 0.7, 0.95]), (N, 8, 1))
    nl[:, :, 0] = alike(rng, both(c), np.where(rng.random((N, 8, V)) < share, -c, c))
    return xx, yy, nl, al
def setup_inputs(rng):
    return pack(*parts(rng))
def setup_inputs_spread(rng):
    s = (N, 8, 16, V)
    xx = np.minimum((16 * np.power(rng.random(s), np.exp2(rng.integers(-3, 4, (N, 8, 1, V))))).astype(np.int64), 15)
    yy = np.where(rng.random(s) < rng.random((N, 8, 1, V)), 1, -1)
    ex = rng.choice(np.array([0.4, 1.0, 2.5]), (N, 8, 1, 1)); ea = rng.choice(np.array([0.4, 1.0, 2.5]), (N, 8, 1, 1))
    nl = np.minimum((W * np.power(rng.random(s), ex)).astype(np.int64), W - 1)
    al = np.minimum((V * np.power(rng.random(s), ea)).astype(np.int64), V - 1)
    return pack(xx, yy, nl, al)
def setup_inputs_ends(rng):
    v = np.arange(V); odd = (np.arange(8) % 2)[None, :, None]; z = ST * (C - 1)
    pat = signs(rng, 1, 8, 16, 1); c = signs(rng, N, 8, V)
    kind = rng.integers(0, 10, (N, 8, V)); kind[..., 1] = 0; kind[..., V - 2] = 0; kind[..., 2] = 2; kind[..., V - 3] = 2; kind[..., V - 1] = 4
    nz = np.where(kind < 2, 16, np.where(kind < 4, 0, rng.integers(7, 10, kind.shape))); nz[..., V - 1] = 8
    o = np.argsort(rng.random((N, 8, 16, V)), axis=2)
    nl = np.where(kind[:, :, None, :] >= 7, rng.integers(0, W, o.shape), np.where(o < nz[:, :, None, :], 0, W - 1))
    nl[..., 0] = np.where((np.arange(16) == 0) | (np.arange(16) > 9), W - 1, 0)
    nl[..., G - 1] = rng.integers(1, G - 1, (N, 8, 16))
    ka = rng.integers(0, 10, (N, 8, V))[:, :, None, :]
    al = np.where(ka < 2, 0, np.where(ka < 4, V - 1, np.where(ka < 7, (V - 1) * rng.integers(0, 2, o.shape), rng.integers(0, V, o.shape))))
    bad = (v % ST < RO) & (rng.random((N, 8, V)) < np.where(odd == 1, 0.9, 0.2))
    bad[..., ST * (C - 2)] = True; bad[..., z:] = False; bad[..., 1] = False; bad[..., 2] = False; bad[..., G - 1] = False; bad[..., 0] = odd[..., 0] == 1
    c = np.where(bad, 1, c); c[..., 0] = 1; c[..., G - 1] = -1; c[..., z] = -c[..., V - 1]
    al = np.where(bad[:, :, None, :], 0, al); al[..., G - 1] = V - 1; al[..., z:] = V - 1; al[:, 0::2, :, 0] = V - 1
    nl[:, :, 0] = np.where(bad, W - 1, nl[:, :, 0]); nl[:, :, 0, z] = np.where(c[..., V - 1] > 0, 0, W - 1)
    kx = rng.integers(0, 5, (N, 8, V))[:, :, None, :]
    xx = np.where(kx == 0, 0, np.where(kx == 1, 15, 15 * rng.integers(0, 2, o.shape)))
    return pack(xx, c[:, :, None, :] * pat, nl, al)
def setup_inputs_corners(rng):
    xx, yy, nl, al = parts(rng); pat = signs(rng, 8, 16, 1)
    cand = np.arange(C) * ST; rest = np.flatnonzero(np.arange(V) % ST != 0); gh = V + np.flatnonzero(np.arange(G) % ST != 0)
    for r in range(N):
        turn = rng.permutation(8); few = int(rng.integers(1, 9))
        for g in range(8):
            nd, nf, nq = ((D, B, Q), (D + 1, B + 1, Q + 1), (C, B + 1, B), (D - 1, B - 1, Q - 1), (few, 16 * few, few), (0, 0, 0), (D, B, 0), (D, 1, 1))[int(turn[g])]
            o = rng.permutation(rest); hp, hm, hq = int(o[0]), int(o[1]), int(o[2])
            c = signs(rng, V); c[cand] = 1; c[hp] = 1; c[hq] = 1; c[hm] = -1; yy[r, g] = c * pat[g]
            nl[r, g, :, hp] = rng.permutation(np.array([hq] * 9 + [hm] * 7))
            will = np.sort(rng.permutation(C)[:nd]) * ST; die = will[:D]; late = will[D:]
            nl[r, g, 0, cand] = hm; nl[r, g, 0, will] = hq; al[r, g][:, cand] = hp
            al[r, g][:, late] = o[rng.integers(3 + nf, len(o), (16, len(late)))]
            if nd == 0: continue
            bs = np.sort(o[3:3 + nf]); m = 16 * len(die)
            al[r, g][:, die] = rng.permutation(np.concatenate([bs, bs[rng.integers(0, nf, m - nf)]])).reshape(16, -1)
            ask = np.zeros(nf, bool); ask[rng.permutation(min(nf, B))[:nq]] = True
            fresh = np.where(ask, gh[rng.integers(0, len(gh), (16, nf))], rest[rng.integers(0, len(rest), (16, nf))])
            dead = die[rng.integers(0, len(die), (16, nf))]
            li = np.where(np.arange(16)[:, None] == rng.integers(0, 16, nf), dead, fresh)
            t = rng.random(nf); li = np.where(~ask & (t < 0.2), fresh, np.where(~ask & (t < 0.3), dead, li))
            nl[r, g][:, bs] = li
    return pack(xx, yy, nl, al)
def setup_inputs_alike(rng):
    xx, yy, nl, al = parts(rng); me = np.arange(V)
    base = rng.integers(0, 16, (N, 8, 16, 4)); base[:, 0] = base[:, 0, :, :1]
    xx = np.take_along_axis(base, rng.integers(0, 4, (N, 8, 1, V)), 3)
    hub = rng.integers(0, W, (N, 8, 24)); hub[..., :4] = np.array([0, V - 1, V, W - 1]); hub[..., 4:8] = ST * np.arange(1, 5); hub[..., 8:12] = V + ST * np.arange(4)
    nl[:, 1::2] = np.take_along_axis(hub[:, 1::2], rng.integers(0, 24, (N, 4, 16 * V)), 2).reshape(N, 4, 16, V)
    nl[:, 2] = np.where(rng.random((N, 16, V)) < 0.3, me, nl[:, 2])
    nl[:, 4] = rng.integers(V, W, (N, 16, V)); nl[:, 6] = rng.integers(0, V, (N, 16, V))
    al[:, 3] = rng.choice(np.array([0, V - 1, V // 2, 3]), (N, 16, V))
    al[:, 5] = np.where(rng.random((N, 16, V)) < 0.5, me, al[:, 5]); al[:, 7] = al[:, 7, :1]
    return pack(xx, yy, nl, al)
def setup_inputs_shared(rng):
    xx, yy, nl, al = parts(rng); pat = signs(rng, 8, 16, 1); v = np.arange(V); K = B // 4; h = K // 2
    cand = np.flatnonzero(v % ST < RO); gh = V + np.flatnonzero(np.arange(G) % ST >= RO)
    q = np.arange(B) // 2 % K; far = np.arange(K) % h % 4 == 3
    for r in range(N):
        for g in range(8):
            m = np.sort(rng.permutation(C)[:2 * K]) * ST + RO; bs = np.stack([m, m + 1], axis=1).reshape(-1)
            o = rng.permutation(np.setdiff1d(v[v % ST >= RO], bs)); hp, hq, hm = int(o[0]), int(o[1]), int(o[2])
            u = o[3:3 + K]; rest = o[3 + K:]; old = rest[:64]; more = np.concatenate([rest, gh])
            die = np.sort(rng.permutation(C)[:D]) * ST
            ws = np.concatenate([rng.permutation(C)[:h] * ST + 1, rng.permutation(C)[:h] * ST + 2])
            c = signs(rng, V); c[cand] = 1; c[hp] = 1; c[hq] = 1; c[hm] = -1; yy[r, g] = c * pat[g]
            nl[r, g, :, hp] = rng.permutation(np.array([hq] * 9 + [hm] * 7))
            nl[r, g, 0, cand] = hm; nl[r, g, 0, die] = hq; nl[r, g, 0, ws] = hq
            al[r, g][:, cand] = hp; al[r, g][:, ws] = old[rng.integers(0, 64, (16, K))]
            al[r, g][:, die] = rng.permutation(np.concatenate([bs, bs[rng.integers(0, B, 16 * D - B)]])).reshape(16, -1)
            base = rng.integers(0, 13, (16, h)); base = np.where(far[:h], 15 * (base & 1), base); base = np.concatenate([base, base], axis=1)
            x = xx[r, g]
            x[:, bs] = base[:, q] + np.where(far[q], 0, rng.integers(0, 2, (16, B)))
            x[:, u] = np.where(far, base, base + 1)
            x[:, ws] = np.where(far, 15 - base, base + 2 * (np.arange(K) >= h))
            lu = np.where(far, u, more[rng.integers(0, len(more), (16, K))]); a = np.where(far, 15, rng.integers(0, 16, K))
            lu[a, np.arange(K)] = ws; lu[(a[:h] + 5) & 15, np.arange(h)] = np.where(far[:h], u[:h], ws[h:])
            nl[r, g][:, u] = lu
            li = more[rng.integers(0, len(more), (16, B))]; a = rng.integers(0, 16, B)
            li[a, np.arange(B)] = die[rng.integers(0, D, B)]; li[(a + rng.integers(1, 16, B)) & 15, np.arange(B)] = u[q]
            nl[r, g][:, bs] = li
    return pack(xx, yy, nl, al)
def check_inputs(d):
    bad = []
    for k, lo, hi in (("xf", 0, 15), ("lab", -1, 1), ("nb", 0, W - 1), ("asc", 0, V - 1)):
        a = np.asarray(d[k]).astype(np.float64)
        if not np.all((a >= lo) & (a <= hi)): bad.append("range of " + k)
        elif k == "xf" and not np.all(a == np.floor(a)): bad.append("xf holds whole numbers")
        elif k == "lab" and not np.all(np.abs(a) == 1): bad.append("lab holds -1 and 1")
    return bad
def take(tab, ix):
    return np.take_along_axis(tab, ix[:, :, None, :], 3)
def alive(lv, names):
    return np.take_along_axis(lv, names.reshape(N, 8, -1), 2).reshape(names.shape)
def apart(X, xb, names):
    return np.stack([np.sum(np.abs(take(X, names[:, :, i]) - xb), axis=2) for i in range(16)], axis=2)
def reference(xf, lab, nb, asc):
    X = both(xf.astype(np.float32).astype(np.int32).reshape(N, 8, 16, V)); Y = both(lab.astype(np.float32).astype(np.int32).reshape(N, 8, 16, V))
    nl = nb.astype(np.int64).reshape(N, 8, 16, V); al = asc.astype(np.int64).reshape(N, 8, 16, V)
    S = np.zeros((N, 8, 16, V), np.int32)
    for i in range(16): S = S + take(Y, nl[:, :, i])
    died = np.zeros((N, 8, V), np.int64); flag = np.zeros((N, 8, V), bool); last = np.zeros(N, np.int64); BIG = 1 << 20
    for t in range(RO):
        v = np.arange(C) * ST + t; av = al[:, :, :, v]
        e = take(Y, nl[:, :, 0, v]) - Y[:, :, :, v]; loss = np.zeros((N, 8, C), np.int64)
        for i in range(16):
            ya = take(Y, av[:, :, i]); sa = take(S, av[:, :, i])
            loss = loss + np.sum(ya * sa > 0, axis=2) - np.sum(ya * (sa + e) > 0, axis=2)
        will = loss <= (last & 7)[:, None, None]
        die = will & (np.add.accumulate(will.astype(np.int64), axis=2) <= D)
        died[:, :, v] = np.where(die, t + 1, died[:, :, v]); last = np.sum(die.astype(np.int64), axis=(1, 2))
        live = died == 0; lv = both(live)
        r, g, i, j = np.nonzero(np.repeat(die[:, :, None, :], 16, axis=2)); flag[r, g, av[r, g, i, j]] = True; flag = flag & live
        tr = flag & (np.add.accumulate(flag.astype(np.int64), axis=2) <= B); flag = flag & ~tr
        b = np.argsort(~tr, axis=2, kind="stable")[..., :B]; ok = np.take_along_axis(tr, b, 2)
        lb = take(nl, b); on = alive(lv, lb); xb = take(X, b)
        k = np.argmax(~on, axis=2); need = ok & np.any(~on, axis=2) & np.any(on, axis=2)
        iu = np.argmin(np.where(on, apart(X, xb, lb), BIG), axis=2); u = np.take_along_axis(lb, iu[:, :, None, :], 2)[:, :, 0]
        asks = need & (u >= V); served = asks & (np.add.accumulate(asks.astype(np.int64), axis=2) <= Q)
        far = take(np.roll(nl, -1, axis=0), np.maximum(u - V, 0)); far = np.where(far < G, V + far, -1)
        lu = np.where((u < V)[:, :, None, :], take(nl, np.minimum(u, V - 1)), far); nm = np.maximum(lu, 0)
        fit = (lu >= 0) & alive(lv, nm) & (lu != b[:, :, None, :]) & ((need & (u < V)) | served)[:, :, None, :]
        for i in range(16): fit = fit & (lu != lb[:, :, i:i + 1])
        iw = np.argmin(np.where(fit, apart(X, xb, nm), BIG), axis=2); w = np.take_along_axis(nm, iw[:, :, None, :], 2)[:, :, 0]
        r, g, s = np.nonzero(np.any(fit, axis=2)); bb = b[r, g, s]; ww = w[r, g, s]; kk = k[r, g, s]; old = nl[r, g, kk, bb]
        nl[r, g, kk, bb] = ww; S[r, g, :, bb] = S[r, g, :, bb] + Y[r, g, :, ww] - Y[r, g, :, old]
        m = ww < V; r, g, bb, ww = r[m], g[m], bb[m], ww[m]
        first = np.unique((r * 8 + g) * V + ww, return_index=True)[1]
        r, g, bb, ww = r[first], g[first], bb[first], ww[first]; al[r, g, (bb + t) & 15, ww] = bb
    return {"yn": nl.reshape(N, 128, V).astype(np.float32), "yd": died.astype(np.float32)}

import numpy as np
from concourse.bass import DstId, RemoteDMATransfer
from concourse.mybir import AluOpType, ActivationFunctionType

F, H, B, I, U = "float32", "float16", "bfloat16", "int32", "uint16"
V_, G_, W_ = 1008, 960, 1968
WIDE = 2216
SB = {
    "NL": ([WIDE], F), "AL": ([WIDE], F), "IOTA": ([WIDE], F), "X": ([1984], B), "Y": ([1984], B),
    "TT": ([WIDE], B), "HH": ([WIDE], B), "DB": ([V_], B), "DD": ([V_], F), "MOD": ([1024], B),
    "NBI": ([V_], I), "ASI": ([V_], I), "NB16": ([V_], U), "G": ([16128], B), "AB": ([V_], B), "NF": ([V_], B),
    "FAR0": ([G_], F), "FAR1": ([G_], F), "FAR2": ([G_], F), "FT": ([G_], F),
    "DM0": ([144], B), "DM1": ([144], B), "DM2": ([144], B), "DI0": ([144], B), "DI1": ([144], B), "DI2": ([144], B),
    "JI": ([1024], I), "JF": ([256], F), "JG": ([256], F), "JM": ([256], F), "J4": ([256], F), "PI": ([8], I), "PC": ([32], F),
    "IB": ([128], B), "NI": ([128], B), "IBIG": ([128], B), "IK": ([128], B), "I16": ([128], F), "OB": ([128], B), "ON": ([128], B),
    "OBIG": ([128], B), "UT": ([128], B), "LT": ([128], B), "ALL": ([128], B), "ZA": ([144], B), "ZK": ([144], B),
    "MM": ([512], B), "RH": ([512], B), "RL": ([512], B), "OFF": ([256], F), "I32": ([128], F), "IN4": ([128], B), "I4": ([128], B), "DG": ([240], F), "CR": ([480], F),
    "MKB": ([240], B), "NKB": ([240], B), "WF": ([240], F), "AF": ([240], F), "ID": ([16], F), "NID": ([16], F),
    "THR": ([240], B), "THF": ([240], F), "RSN": ([240], F), "DIAG": ([64], F), "SLOT": ([16], F), "DUM": ([16], F), "JB": ([240], B), "R2": ([256], B),
    "RST": ([240], F), "NST": ([240], F), "ONE": ([144], F), "TMP": ([256], F),
    "AV16": ([144], U), "GT": ([2304], B), "N0": ([144], H), "N16": ([16], U), "YN": ([144], B), "XB": ([240], B), "YW": ([240], B), "L2": ([240], U), "SF": ([64], F), "AC": ([240], B), "NG": ([240], B), "E2": ([144], F), "EH": ([144], F),
    "CC": ([144], F), "RR": ([144], F), "A1": ([144], H), "A2": ([144], H), "WILL": ([144], F), "CUM": ([144], F),
    "JUNK": ([432], B), "ACC": ([4], F), "DL16": ([4], U), "LE": ([144], F), "EC": ([8], B), "EI": ([8], I), "TH": ([8], F),
    "AVP": ([144], H), "HP": ([144], H), "HL": ([512], B), "OH": ([4096], B), "CN": ([256], B), "PR": ([32], B), "FLAG": ([64], B), "FL": ([64], B),
    "CU": ([64], F), "PT": ([128], F), "CM": ([128], F), "CQ": ([960], B), "CB": ([48], F), "CB16": ([16], U), "FN": ([240], B),
    "B16": ([16], U), "BF": ([16], F), "BS": ([48], F), "BS16": ([16], U), "BT16": ([16], U), "BR": ([15, 16], F),
    "LB": ([256], F), "LU": ([256], F), "L16": ([240], U), "XR": ([3840], B), "LH": ([8, 32], H), "LX": ([8, 32], H),
    "D": ([3840], B), "DA": ([15, 16, 16], B), "LBT": ([15, 32], F), "NR2": ([240], F), "K2": ([240], F), "SC": ([480], F),
    "MI": ([32], I), "NM": ([32], I), "KI": ([16], I), "U16": ([32], U), "K16": ([16], U), "SM": ([256], F), "ASK": ([32], B),
    "EQ": ([4080], B), "W16": ([16], U), "WI": ([32], I), "WD16": ([16], U), "WS16": ([16], U),
    "MK": ([240], F), "LBM": ([240], F), "NEW": ([240], F), "A0": ([240], B), "YO": ([240], B), "YB": ([240], B), "HB": ([240], B),
    "HN": ([240], B), "MR": ([240], B), "BV": ([240], F), "AG": ([240], F), "WR": ([240], H),
    "E3": ([15, 240], B), "DUP": ([480], F),
}
SIZE = {F: 4, H: 2, B: 2, I: 4, U: 2}
ALIAS = {}
_at = {}
for _k in list(SB):
    _sh, _dt = SB[_k]
    if _k in ("GT", "OH", "D", "EQ", "CQ"):
        _ar = "G"
    elif len(_sh) == 1 and _sh[0] <= 512 and _k[:2] not in ("DM", "DI"):
        _ar = "S" + _dt
    else:
        continue
    _u = 32 // SIZE[_dt]
    ALIAS[_k] = (_ar, _at.get(_ar, 0), _sh[0])
    _at[_ar] = _at.get(_ar, 0) + (_sh[0] + _u - 1) // _u * _u
    del SB[_k]
    if _ar != "G":
        SB[_ar] = ([_at[_ar]], _dt)
SCRATCH = {k: ("sbuf", [128] + v[0], v[1]) for k, v in SB.items()}
for _k in range(8):
    SCRATCH["P%d" % _k] = ("psum", [128, 512], F)
MSGS = ["Y", "X", "N0", "D0", "N1", "D1", "N2", "D2"]
SEMAPHORES = (["ev", "es", "ep", "eg", "ly", "lx", "lnb", "las", "lmod", "oyn", "oyd"]
              + ["a" + m for m in MSGS] + ["l" + m for m in MSGS])
S_ = np.s_
AL_, AF = AluOpType, ActivationFunctionType
K_ = 32768.0
GATH, SCAT, WAKE = 1.62, 3.95, 60
BON = 15.0
LATE = 1e6
LAZY = ("DB", "X", "EC", "FT", "DD", "EI", "TH", "SF", "FLAG", "BF", "BS", "BS16", "BT16", "BR", "LBT", "NR2", "LBM", "MKB", "NKB", "YO", "HB",
        "YB", "MR", "MK", "BV", "HN", "HH")
TURNS, SHAKE = 40, 500.0
PLAN = []
SPLIT_B, SPLIT_D = 160, 112


def bits(engines):
    m = 0
    for e in engines:
        m |= 1 << e
    return m


def paths(src, dst, topo):
    ok = [c for c in topo.cores_of(src) if topo.may_write(c, dst)]
    near = sorted([c for c in ok if topo.die(c) == topo.die(src)], key=lambda c: c != src)
    far = [c for c in ok if topo.die(c) != topo.die(src)]
    return near[:2] + far[:2]


def message(m):
    if m in ("X", "Y"):
        return m, m, V_, G_, 4
    if m[0] == "N":
        return "NL", "FAR" + m[1], 0, G_, 4
    return "DM" + m[1], "DI" + m[1], 0, 144, 1


def first_masks(src, dst, n, topo):
    ps = paths(src, dst, topo)[:n]
    used, out = [], []
    for p in ps:
        can = [e for e in topo.engines(src, dst if p == src else p) if e not in used]
        take = can if n == 1 else can[:4]
        used += take
        out.append(take)
    return ps, out


def relay_program(g, core, T, topo):
    n = len(T.cores)
    for r in range(n):
        src, dst = T.cores[r], T.cores[(r - 1) % n]
        if core not in topo.cores_of(src):
            continue
        rid, pid = topo.addr(dst, core)
        for m in MSGS:
            _, land, c0, cols, k = message(m)
            ps, ms = first_masks(src, dst, k, topo)
            if core not in ps:
                continue
            j = ps.index(core)
            w = cols // k
            ap = T[land][:, c0 + j * w:c0 + (j + 1) * w]
            g.wait_ge(T.sem["a" + m], len(ms[j]))
            g.remote_dma(ap, ap, T.sem["a" + m], T.sem["l" + m], pid, rid, topo.mask(core, dst))
        for m in MSGS:
            if core in paths(src, dst, topo)[:message(m)[4]]:
                g.wait_ge(T.sem["l" + m], len(topo.engines(core, dst)))


def rank_program(g, core, T, topo):
    rank = T.rank_of(core)
    if rank is None:
        relay_program(g, core, T, topo)
        return
    n = len(T.cores)
    prev, nxt = T.cores[(rank - 1) % n], T.cores[(rank + 1) % n]
    ops = []

    def A(name, idx=S_[:, ...]):
        own = name
        if name in ALIAS:
            name, c0, size = ALIAS[name]
            rg = range(c0, c0 + size)[slice(None) if idx[1] is Ellipsis else idx[1]]
            idx = (idx[0], slice(rg[0], rg[-1] + 1, None if rg.step == 1 else rg.step))
        where, shape, dt_ = SCRATCH[name]
        ix = [i for i in idx[1:] if i is not Ellipsis]
        lo = hi = 0
        cnt = 1
        stride = int(np.prod(shape[1:]))
        for d, size in enumerate(shape[1:]):
            stride //= size
            i = ix[d] if d < len(ix) else slice(None)
            rg = range(size)[i] if isinstance(i, slice) else [i]
            lo += rg[0] * stride
            hi += rg[-1] * stride
            cnt *= len(rg)
        sz, per = SIZE[dt_], None
        if len(rg) > 1 and rg.step > 1:
            per = (rg.step * sz, rg[0] % rg.step * sz, (rg[0] % rg.step + 1) * sz)
        elif len(shape) > 2 and len(rg) < shape[-1]:
            per = (shape[-1] * sz, rg[0] * sz, (rg[-1] + 1) * sz)
        if idx[-1] is Ellipsis:
            idx = slice(None)
        if where == "psum":
            return ("@", T[name][idx], [(name, 0, 2048, None)], [], cnt, 8, own)
        return ("@", T[name][idx], [(name, lo * sz, (hi + 1) * sz, per)], [], cnt, sz, own)

    def C(name, a, b=None, step=None):
        return A(name, S_[:, a:(a + 1 if b is None else b):step])

    def IN(win, off):
        return ("@", win[1].indirect(off[1]), win[2], off[2], 16 * off[4], 0, win[6])

    def isd(x):
        return isinstance(x, tuple) and len(x) == 7 and x[0] == "@"

    def call(q, fn, *args, **kw):
        rd, wr = [], []
        for k, x in list(enumerate(args)) + list(kw.items()):
            if isd(x):
                (wr if k in (0, "accum_out") else rd).extend(x[2])
                rd.extend(x[3])
        a2 = [x[1] if isd(x) else x for x in args]
        k2 = {k: (x[1] if isd(x) else x) for k, x in kw.items()}
        o, src = args[0], [x for x in args[1:] if isd(x) and x[4] == args[0][4]]
        if o[5] == 0:
            c = 50 + SCAT * o[4]
        elif any(x[5] == 0 for x in src):
            c = 50 + GATH * o[4]
        elif q == "g":
            c = 130 + 2.1 * o[4]
        elif q == "s":
            c = 15 + 1.04 * max(64, o[4])
        elif len(src) == 2 and len(args) == 4:
            c = 1.04 * max(64, o[4] * (1 if 8 in (src[0][5], src[1][5]) else 2))
        else:
            c = 1.04 * max(64, o[4] * (0.5 if o[5] == 2 and all(x[5] == 2 for x in src[:1]) else 1))
        ops.append({"q": q, "f": lambda: fn(*a2, **k2), "r": rd, "w": wr, "d": None, "c": c, "l": 0,
                    "k": len(ops) + (LATE if o[6] in LAZY or (o[6] == "NL" and q == "s") else 0)})

    def dma(q, fn, rd, wr, sem, cnt, busy=60, lat=2500):
        ops.append({"q": q, "f": fn, "r": rd, "w": wr, "d": (sem, cnt), "c": busy, "l": lat, "k": len(ops)})

    def cp(o, i): call("v", g.vector.tensor_copy, o, i)
    def tt(o, a, b, op): call("v", g.vector.tensor_tensor, o, a, b, op)
    def ms(o, c): call("v", g.vector.memset, o, c)
    def scan(o, a, b, op0, op1): call("v", g.vector.tensor_tensor_scan, o, a, b, 0.0, op0, op1)
    def act(o, i, f=AF.Identity, **kw): call("s", g.scalar.activation, o, i, f, **kw)

    def mv(o, i):
        act(o, i)
        other = ops.pop()
        cp(o, i)
        ops[-1]["or"] = other

    group = {}

    def mm(o, l, r, st, sp=None):
        bank = o[2][0][0]
        if st:
            group[bank] = len(ops)
        ops.append({"q": "p", "f": lambda stop: g.tensor.matmul(o[1], l[1], r[1], st, stop), "r": l[2] + r[2], "w": o[2], "d": None,
                    "c": 0.52 * max(min(64, l[4]), r[4]) * (4 if l[5] == 4 else 1), "l": 60, "g": group[bank], "st": st,
                    "k": len(ops) + (LATE if r[6] in LAZY + ("LB",) else 0)})

    def rank_as(first, at):
        for i, o in enumerate(ops[first:]):
            o["k"] = at + 1e-4 * i

    def ts(o, a, s1, op0, s2=None, op1=None):
        if op1 is None:
            call("v", g.vector.tensor_scalar, o, a, s1, None, op0)
        else:
            call("v", g.vector.tensor_scalar, o, a, s1, s2, op0, op1)

    def iota(o, pat, base, cm, fl=True):
        if fl:
            call("g", g.iota, o, pat, base, cm, allow_small_or_imprecise_dtypes=True)
        else:
            call("g", g.iota, o, pat, base, cm)

    def send(m):
        srcb, land, c0, cols, k = message(m)
        ps, mk = first_masks(core, prev, k, topo)
        w = cols // k
        tr = []
        for j, p in enumerate(ps):
            to = prev if p == core else p
            rid, pid = topo.addr(to, core)
            tr.append(RemoteDMATransfer(dst_ids=[DstId(rid=rid, pnc=pid)], dma_engine_mask=bits(mk[j]), remote_sem=T.sem["a" + m],
                                        src=T[srcb][:, j * w:(j + 1) * w], dst=T[land][:, c0 + j * w:c0 + (j + 1) * w]))
        dma("g", lambda: g.remote_dma_fused(tr, local_sem=T.sem["l" + m]), C(srcb, 0, cols)[2], [], "l" + m, -sum(len(x) for x in mk), 500, 3000)
        ops[-1]["sent"] = m

    def arrive(m):
        _, land, c0, cols, k = message(m)
        ps, mk = first_masks(nxt, core, k, topo)
        cnt = sum(len(mk[j]) if p == nxt else len(topo.engines(p, core)) for j, p in enumerate(ps))
        dma(None, None, [], C(land, c0, c0 + cols)[2], "a" + m, -cnt, 0, 5500 if k == 1 else 13000 if m[0] == "N" else 7500)
        ops[-1]["comes"] = m

    def sel(z, s):
        return C(z, 15 - s, 143 - s)

    add, sub, mul, mx, mn = AL_.add, AL_.subtract, AL_.mult, AL_.max, AL_.min
    eq, ge, gt, le, lt = AL_.is_equal, AL_.is_ge, AL_.is_gt, AL_.is_le, AL_.is_lt
    shr, band = AL_.arith_shift_right, AL_.bitwise_and

    for m in MSGS:
        arrive(m)
    dma("y", lambda: g.sync.dma_start(T.Y[:, 0:V_], T.lab[:]), [], C("Y", 0, V_)[2], "ly", 16, 60, 3500)
    dma("y", lambda: g.sync.dma_start(T.NBI[:], T.nb[:]), [], A("NBI")[2], "lnb", 16, 60, 5200)
    dma("y", lambda: g.sync.dma_start(T.X[:, 0:V_], T.xf[:]), [], C("X", 0, V_)[2], "lx", 16, 60, 4000)
    dma("y", lambda: g.sync.dma_start(T.ASI[:], T.asc[:]), [], A("ASI")[2], "las", 16, 60, 8000)
    iota(C("JI", 0, 256), [[1, 256]], 0, 0, False)
    iota(C("PI", 0), [[1, 1]], 0, 1, False)
    send("Y")
    send("X")
    consts = len(ops)
    iota(A("IOTA"), [[1, WIDE]], 0, 0)

    J = C("JI", 0, 256)
    ts(C("JI", 256, 512), J, 4, shr)
    ts(C("JI", 512, 768), J, 15, band)
    ts(C("JI", 768, 1024), J, 2, shr)
    ts(C("PI", 1), C("PI", 0), 4, shr)
    ts(C("PI", 2), C("PI", 0), 15, band)
    ts(C("PI", 3), C("PI", 0), 4, shr, 1, band)
    cp(A("JF"), J)
    cp(A("JG"), C("JI", 256, 512))
    cp(A("JM"), C("JI", 512, 768))
    cp(A("J4"), C("JI", 768, 1024))
    cp(C("PC", 0, 4), C("PI", 0, 4))
    P, PG, PM, PA = C("PC", 0), C("PC", 1), C("PC", 2), C("PC", 3)
    J128, G128, M128 = C("JF", 0, 128), C("JG", 0, 128), C("JM", 0, 128)
    ts(A("IB"), J128, P, eq)
    ts(A("NI"), J128, P, eq, -1.0, mul)
    ms(C("X", W_, 1984), 31.0)
    ms(C("Y", W_, 1984), 0.0)
    ts(C("PC", 4), PG, 16.0, mul, 15.0, add)
    ts(C("PC", 5), PM, 0.0, eq)
    ts(C("PC", 6), P, 16.0, add)
    ts(C("PC", 7), P, -16.0, add)
    ts(C("PC", 8), PA, -1.0, mul, 1.0, add)
    ts(C("PC", 9), PM, 8.0, lt)
    ts(C("PC", 10), PM, 8.0, ge)
    ts(C("PC", 11), PG, 8.0, mul, PM, add)
    ts(C("PC", 12), C("PC", 11), -8.0, add)
    ts(A("SLOT"), C("JF", 0, 16), 16.0, mul, PM, add)
    ts(A("ID"), C("JF", 0, 16), PM, eq)
    ts(C("PC", 13, 16), C("SLOT", 0, 3), 0.5, add)
    ts(A("DUM"), A("SLOT"), 1969.0, add)
    ts(A("NID"), A("ID"), -1.0, mul, 1.0, add)
    ms(C("PC", 16, 19), 1.0)
    ts(C("PC", 19), PM, 14.0, eq, 60.0, mul)
    ts(C("PC", 19), C("PC", 19), 1.0, add)
    cp(A("NB16"), A("NBI"))
    ts(A("ZA"), C("JF", 0, 144), C("PC", 4), eq)
    ts(A("ZK"), C("JF", 0, 144), C("PC", 4), eq, K_, mul)
    ts(A("OB"), G128, PG, eq)
    ts(A("ON"), G128, PG, eq, -1.0, mul)
    ts(A("OBIG"), G128, PG, eq, 2.0 ** 18, mul)
    ts(A("IBIG"), J128, P, eq, 2.0 ** 23, mul)
    ts(A("IK"), J128, P, eq, 1024.0, mul)
    ts(A("I16"), J128, P, eq, 16.0, mul)
    ts(C("TMP", 0, 128), M128, PM, lt)
    ts(C("TMP", 128, 256), M128, PM, ge)
    tt(A("UT"), C("TMP", 0, 128), A("OB"), mul)
    tt(A("LT"), C("TMP", 128, 256), A("OB"), mul)
    ms(A("ALL"), 1.0 / 16)
    ms(A("ONE"), 1.0)
    for a in range(2):
        for h in range(2):
            ts(C("MM", 128 * (2 * a + h), 128 * (2 * a + h + 1)), J128, P if a == h else C("PC", 6 + a), eq, PA if a else C("PC", 8), mul)
    for h in range(2):
        ts(C("RH", 256 * h, 256 * h + 256), A("J4"), C("PC", 11 + h), eq, C("PC", 9 + h), mul)
    act(A("RL"), A("RH"), scale=-32.0)
    act(A("I32"), A("IB"))
    act(A("IN4"), A("IB"), scale=-4096.0)
    act(A("I4"), A("IB"), scale=4096.0)
    ts(A("DG"), C("JM", 0, 240), PM, eq)
    cp(C("NL", 0, V_), A("NBI"))
    send("N0")
    iota(C("NL", W_, WIDE), [[0, WIDE - W_]], W_, 0)
    iota(C("AL", V_, WIDE), [[0, WIDE - V_]], 1023, 0)
    iota(C("HH", V_, WIDE), [[0, WIDE - V_]], 0, 0)
    iota(A("DD"), [[0, V_]], 0, 0)
    for s4 in range(4):
        ms(C("OFF", s4, 128, 4), -1025.0 - 4 * s4)
        ms(C("OFF", 128 + s4, 256, 4), 32800.0 - 4 * s4)
    ts(C("TMP", 96, 128), C("JM", 0, 32), 2.0, mul)
    tt(C("TMP", 128, 160), C("TMP", 96, 128), C("JG", 0, 32), add)
    ts(A("PR"), C("TMP", 128, 160), P, eq)
    M240 = C("JM", 0, 240)
    ts(A("R2"), A("JM"), 2048.0, mul)
    ts(A("RST"), M240, 0.0, eq, 1e9, mul)
    ts(A("NST"), M240, 0.0, AL_.not_equal)
    ts(A("DIAG"), C("JM", 0, 64), PM, eq)
    cp(A("JB"), C("JF", 0, 240))
    ms(C("TMP", 0, 16), 0.5)
    ms(C("TMP", 16, 32), 0.0)
    call("v", g.vector.tensor_tensor_scan, C("TMP", 32, 48), C("TMP", 0, 16), C("TMP", 16, 32), 2.0 ** 29, mul, add)
    tt(C("TMP", 48, 64), C("TMP", 32, 48), A("ID"), mul)
    scan(C("TMP", 64, 80), C("ONE", 0, 16), C("TMP", 48, 64), mul, add)
    cp(C("PC", 20), C("TMP", 79))
    ts(C("PC", 21), C("TMP", 79), -2.5, mul)
    ts(A("THF"), M240, PM, AL_.not_equal, -2.0 ** 62, mul)
    ts(A("THR"), A("THF"), C("PC", 21), add)
    ts(A("RSN"), A("RST"), -1e20, mul)
    cp(C("AL", 0, V_), A("ASI"))
    iota(A("DB"), [[0, V_]], 0, 0)
    ts(C("MOD", 0, 256), A("JM"), PM, eq)
    for k in range(1, 4):
        dma("y", lambda k=k: g.sync.dma_start(T.MOD[:, 256 * k:256 * (k + 1)], T.MOD[:, 0:256]),
            C("MOD", 0, 256)[2], C("MOD", 256 * k, 256 * (k + 1))[2], "lmod", 16)
    ms(A("FLAG"), 0.0)
    ms(A("AVP"), 0.0)
    ms(A("HP"), 0.0)
    ms(A("CU"), 9999.0)
    ms(A("PT"), 9999.0)
    ms(C("LB", 240, 256), 1968.0)
    ms(C("LU", 240, 256), 1968.0)

    rank_as(consts, LATE)
    Yw, Xw, NLw = C("Y", 0, 1984), C("X", 0, 1984), C("NL", 0, 1976)

    def eps_first(t):
        ts(A("N0"), C("NL", t, V_, 7), C("PC", 5), mul)
        for s in range(16):
            mm(C("P5", 0, 9), sel("ZA", s), C("N0", s, 144, 16), s == 0, s == 15)

    def eps_second(t):
        cp(C("N16", 0, 9), C("P5", 0, 9))
        mv(A("YN"), IN(Yw, C("N16", 0, 9)))
        e = C("P5", 16, 160)
        mm(e, A("IB"), A("YN"), True)
        mm(e, A("NI"), C("Y", t, V_, 7), False)
        act(A("E2"), e, AF.Square, scale=4.0)
        act(A("EH"), e, AF.Square, scale=4.0, bias=1.0 / 16)
        act(A("CC"), A("EH"), bias=-1.0 / 256)

    eps_first(0)

    def code(k):
        a, b = 256 * k, min(256 * k + 256, V_)
        act(C("AB", a, b), C("P%d" % k, 0, b - a), AF.Abs, bias=-1.0 / 64)
        mv(C("HH", a, b), C("P%d" % k, 0, b - a))
        ts(C("NF", a, b), C("AB", a, b), 2.0, mn, 2.0, sub)
        tt(C("TT", a, b), C("NF", a, b), C("Y", a, b), mul)
        ops[-1]["b"] = 13.0 * (V_ - b) + (3000.0 if k < 3 else 0.0)

    eps_second(0)
    for k in range(4):
        a0, b0 = 256 * k, min(256 * k + 256, V_)
        mm(C("P%d" % k, 0, b0 - a0), A("NI"), C("Y", a0, b0), True)
        for a in range(a0, b0, 64):
            b = min(a + 64, V_)
            for c in range(a, b, 32):
                mv(C("G", 16 * c, 16 * min(c + 32, b)), IN(Yw, C("NB16", c, min(c + 32, b))))
                ops[-1]["b"] = 13.0 * (V_ - c)
            for r in range(16):
                mm(C("P%d" % k, a - a0, b - a0), A("IB"), C("G", 16 * a + r, 16 * b, 16), False)
        code(k)

    def transpose(src):
        cp(A("LH", S_[:, :, 0:16]), C(src, 0, 128))
        cp(A("LH", S_[:, :, 16:32]), C(src, 128, 256))
        call("v", g.vector.transpose, A("LX"), A("LH"))

    def names(bank, c0, first):
        for a in range(2):
            for h in range(2):
                mm(C(bank, c0 + 128 * a, c0 + 128 * a + 128), C("MM", 128 * (2 * a + h), 128 * (2 * a + h + 1)),
                   A("LX", S_[:, :, 16 * h:16 * h + 16]), first and h == 0)

    def distances(lst, split):
        for a in range(0, split, 32):
            b = min(a + 32, split)
            tt(C("D", 16 * a, 16 * b), IN(Xw, C(lst, a, b)), C("XR", 16 * a, 16 * b), sub)
            ops[-1]["b"] = BON * (240 - a)
            act(A("DA", S_[:, a // 16:b // 16, :, :]), C("D", 16 * a, 16 * b), AF.Abs)
        for k, a in enumerate(range(split, 240, 32)):
            b = min(a + 32, 240)
            diff = C("P%d" % (1 + k % 4), 0, 16 * (b - a))
            act(C("D", 16 * a, 16 * b), IN(Xw, C(lst, a, b)))
            ops[-1]["b"] = BON * (240 - a + split)
            mm(diff, A("IB"), C("D", 16 * a, 16 * b), True)
            mm(diff, A("NI"), C("XR", 16 * a, 16 * b), False)
            act(A("DA", S_[:, a // 16:b // 16, :, :]), diff, AF.Abs)
        for lo, hi in ((0, split // 16), (split // 16, 15)):
            for c0 in range(lo, hi, 4):
                c1 = min(c0 + 4, hi)
                for s in range(16):
                    mm(C("P0", 16 * c0, 16 * c1), sel("ZK", s), A("DA", S_[:, c0:c1, s, :]), False)

    for t in range(3):
        tn = str(t)
        DM = A("DM" + tn)
        if t == 0:
            cp(A("AV16"), C("AL", t, V_, 7))
        for c in range(0, 144, 36):
            mv(C("GT", 16 * c, 16 * c + 576), IN(C("TT", 0, V_), C("AV16", c, c + 36)))
        for hf in range(2):
            for r in range(16):
                mm(C("P0", 72 * hf, 72 * hf + 72), A("IB"), C("GT", 1152 * hf + r, 1152 * hf + 1152, 16), r == 0)
        x = C("P0", 0, 144)
        ts(A("RR"), x, 12582912.0, add, 12582912.0, sub)
        tt(A("A1"), x, A("E2"), mul)
        tt(A("A2"), A("RR"), A("CC"), mul)
        mm(C("P2", 0, 144), A("ON"), A("A1"), True, False)
        mm(C("P2", 0, 144), A("OB"), A("A2"), False, True)
        ts(A("WILL"), C("P2", 0, 144), 0.0 if t == 0 else C("TH", 0), le)
        scan(A("CUM"), A("ONE"), A("WILL"), mul, add)
        for e in range(3):
            act(C("JUNK", 144 * e, 144 * e + 144), A("CUM"), AF.Sign, scale=-1.0, bias=C("PC", 13 + e), accum_out=C("ACC", e))
        ts(A("LE"), A("CUM"), 48.5, le, 31.0, mul)
        tt(DM, A("LE"), A("WILL"), mul)
        send("D" + tn)
        act(C("DB", t, V_, 7), DM, scale=-2.0)
        tt(C("X", t, V_, 7), C("X", t, V_, 7), DM, mx)
        ts(C("DL16", 0, 3), C("ACC", 0, 3), 3.5, mul, 504.0 + t, add)
        ALw = C("AL", 0, 1016)
        ts(C("HP", 48, 96), IN(ALw, C("DL16", 0, 3)), 1.0 / 32, mul, 1025.0 - 15.5 / 32, add)
        cp(C("AVP", 48, 96), IN(ALw, C("DL16", 0, 3)))
        for hf in range(2):
            bank = "P%d" % (3 - 2 * hf)
            for h in range(2):
                c0 = 256 * h + 128 * hf
                mm(A(bank, S_[0:96, 0:128]), C("HP", 48 - 48 * h, 144 - 48 * h), C("RH", c0, c0 + 128), h == 0)
            for h in range(2):
                c0 = 256 * h + 128 * hf
                mm(A(bank, S_[0:96, 128:256]), C("HP", 48 - 48 * h, 144 - 48 * h), C("RL", c0, c0 + 128), h == 0)
                mm(A(bank, S_[0:96, 128:256]), C("AVP", 48 - 48 * h, 144 - 48 * h), C("RH", c0, c0 + 128), False)
            tt(A("HL", S_[0:96, 256 * hf:256 * hf + 256]), A(bank, S_[0:96, 0:256]), A("OFF", S_[0:96, :]), add)
        hist = C("P4", 0, 63)
        mm(C("P4", 0, 64), A("IB"), A("FLAG"), True)
        for s in range(16):
            mm(hist, sel("ZA", s), C("DB", s, V_, 16), False, False)
        if t < 2:
            ts(C("EC", 0), C("CUM", 143), 48.0, mn)
        for c in range(0, G_, 240):
            act(C("FT", c, c + 240), C("FAR" + tn, c, c + 240), AF.Relu, scale=-1.0, bias=960.0)
            act(C("NL", V_ + c, V_ + c + 240), C("FT", c, c + 240), scale=-1.0, bias=1968.0)
        for hf in range(2):
            for j in range(8):
                ts(A("OH", S_[0:96, 2048 * hf + j:2048 * hf + 2048:8]), A("HL", S_[0:96, 256 * hf:256 * hf + 256]), float(16 * (j % 2) + j // 2), eq)
                ops[-1]["b"] = 1500.0 * (1 - hf)
            bank = "P%d" % (2 + 5 * hf)
            for col in range(32):
                c0 = 2048 * hf + 32 * col
                mm(A(bank, S_[0:32, 32 * (col // 8):32 * (col // 8) + 32]), A("OH", S_[0:96, c0:c0 + 32]),
                   A("OH", S_[0:96, c0 + 1024:c0 + 1056]), col % 8 == 0)
            mv(A("CN", S_[0:32, 128 * hf:128 * hf + 128]), A(bank, S_[0:32, 0:128]))
        for c0 in range(2):
            mm(C("P4", c0, 64, 2), A("CN", S_[0:32, c0:256:2]), A("PR", S_[0:32, 0:32]), False)
        if t < 2:
            mm(C("P1", 0), A("ALL"), C("EC", 0), True, True)
        ng = len(range(t, G_, 7))
        act(C("DD", t, V_, 7), DM, AF.Relu, bias=t - 30.0)
        if t == 2:
            dma("y", lambda: g.sync.dma_start(T.yd[:], T.DD[0:128:16, :]), A("DD")[2], [], "oyd", 16)
        tt(C("X", V_ + t, W_, 7), C("X", V_ + t, W_, 7), C("DI" + tn, 0, ng), mx)
        FL = C("FL", 0, 63)
        ts(FL, hist, 0.5, gt)
        mm(C("P5", 0, 63), A("OB"), FL, True, True)
        mm(C("P5", 64, 127), A("UT"), FL, True, True)
        if t < 2:
            cp(C("EI", 0), C("P1", 0))
            ts(C("EI", 1), C("EI", 0), 7, band)
            ts(C("TH", 0), C("EI", 1), 2.0, mul)
        scan(C("CU", 0, 63), C("ONE", 0, 63), C("P5", 0, 63), mul, add)
        tt(C("CM", 0, 64), A("CU"), A("DIAG"), mul)
        tt(C("PT", 0, 63), C("CU", 0, 63), C("P5", 64, 127), sub)
        scan(C("CM", 64, 128), C("NST", 0, 64), C("CM", 0, 64), mul, add)
        for q in range(4):
            ts(C("CQ", 240 * q, 240 * q + 240), A("JB"), C("CM", 79 + 16 * q), ge, C("PC", 16 + q), mul)
            mm(C("P6", 256, 496), A("OB"), C("CQ", 240 * q, 240 * q + 240), q == 0)
        if t < 2:
            ts(C("SF", 0, 63), C("PT", 0, 63), 240.5, gt)
            tt(C("FLAG", 0, 63), C("SF", 0, 63), FL, mul)
        tt(C("CR", 0, 240), C("P6", 256, 496), A("DG"), mul)
        scan(C("CR", 240, 480), A("NST"), C("CR", 0, 240), mul, add)
        cp(C("CB16", 0, 15), C("CR", 255, 480, 16))
        mm(C("P6", 32, 47), A("I16"), C("CR", 255, 480, 16), True)
        tt(A("FN"), IN(A("PT"), C("CB16", 0, 15)), C("JF", 0, 240), le)
        for s in range(16):
            mm(C("P6", 32, 47), sel("ZA", s), C("FN", s, 240, 16), False, s == 15)
        b16, bf = C("B16", 0, 15), C("BF", 0, 15)
        cp(b16, C("P6", 32, 47))
        act(A("XB"), IN(Xw, b16))
        cp(A("L16"), IN(NLw, b16))
        cp(bf, C("P6", 32, 47))
        act(C("LB", 0, 240), IN(NLw, b16))
        for k in range(16):
            cp(C("XR", k, 3840, 16), A("XB"))
        mm(C("P0", 0, 256), A("IB"), A("R2"), True)
        transpose("LB")
        names("P7", 0, True)
        names("P0", 0, False)
        first = len(ops)
        mm(C("P6", 256, 512), A("IB"), A("R2"), True)
        mm(C("P6", 256, 512), A("IB"), A("R2"), False)
        names("P6", 256, False)
        names("P6", 256, False)
        rank_as(first, LATE + first)
        distances("L16", SPLIT_B)
        mv(A("LBT", S_[:, :, 0:16]), C("P7", 0, 240))
        mv(A("LBT", S_[:, :, 16:32]), C("P7", 0, 240))
        mv(A("NR2"), C("P6", 256, 496))
        mv(A("BR", S_[:, :, 0]), bf)
        for k in (1, 2, 4, 8):
            mv(A("BR", S_[:, :, k:2 * k]), A("BR", S_[:, :, 0:k]))
        ts(C("BS", 0, 15), bf, 1968.0, ge)
        tt(C("BS", 16, 31), C("BS", 0, 15), C("SLOT", 0, 15), mul)
        tt(C("BS", 32, 47), C("BS", 16, 31), bf, add)
        bs16 = C("BS16", 0, 15)
        cp(bs16, C("BS", 32, 47))
        if t < 2:
            ts(C("BT16", 0, 15), bf, float(t), add, 1023.0, mn)
        PK = C("P0", 0, 240)
        scan(C("SC", 0, 240), A("RST"), PK, add, mn)
        cp(C("MI", 0, 15), C("SC", 15, 240, 16))
        ts(C("NM", 0, 15), C("MI", 0, 15), 2047, band)
        u16, o16 = C("U16", 0, 15), C("U16", 16, 31)
        cp(u16, C("NM", 0, 15))
        cp(A("L2"), IN(NLw, u16))
        act(C("LU", 0, 240), IN(NLw, u16))
        tt(A("K2"), A("NR2"), PK, sub)
        scan(C("SC", 240, 480), A("RST"), A("K2"), add, mn)
        cp(C("MI", 16, 31), C("SC", 255, 480, 16))
        ts(C("NM", 16, 31), C("MI", 16, 31), 2047, band)
        mm(C("P0", 0, 256), A("IB"), A("R2"), True)
        ts(C("KI", 0, 15), C("MI", 16, 31), 11, shr, 15, band)
        ts(C("SM", 0, 15), C("SC", 15, 240, 16), 250 * K_, lt)
        ts(C("SM", 16, 31), C("SC", 255, 480, 16), -248 * K_, lt)
        transpose("LU")
        names("P7", 0, True)
        names("P0", 0, False)
        distances("L2", SPLIT_D)
        ts(C("SM", 32, 47), C("NM", 0, 15), 1008.0, ge)
        tt(C("SM", 48, 63), C("SM", 0, 15), C("SM", 16, 31), mul)
        cp(o16, C("NM", 16, 31))
        cp(C("K16", 0, 15), C("KI", 0, 15))
        ts(C("SM", 64, 79), C("NM", 16, 31), 250 * K_, add)
        tt(C("ASK", 0, 15), C("SM", 32, 47), C("SM", 48, 63), mul)
        ts(C("ASK", 16, 31), C("SM", 48, 63), -2.0, mul, 1.0, add)
        cnt = C("P5", 0, 15)
        mm(cnt, A("LT"), C("ASK", 0, 15), True, False)
        mm(cnt, A("IK"), C("ASK", 0, 15), False, False)
        for d in range(1, 15):
            mm(C("P5", d, 15), A("OB"), C("ASK", 0, 15 - d), False, False)
        mm(cnt, A("IK"), C("ASK", 16, 31), False, True)
        ts(C("SM", 80, 95), cnt, 48.5, gt, 256 * K_, mul)
        lbm = C("P6", 256, 496)
        mm(lbm, A("I32"), C("LB", 0, 240), True)
        if t == 2:
            mv(A("MKB"), IN(A("ID"), C("K16", 0, 15)))
            mm(lbm, A("IN4"), A("MKB"), False)
            act(A("LBM"), lbm)
        else:
            mv(A("NKB"), IN(A("NID"), C("K16", 0, 15)))
            mm(lbm, A("I4"), A("NKB"), False)
            act(A("LBM"), lbm, bias=-4096.0)
            mv(A("YO"), IN(Yw, o16))
            mv(A("HB"), IN(A("HH"), bs16))
            mv(A("YB"), IN(Yw, b16))
            mv(A("MR"), IN(A("MOD"), C("BT16", 0, 15)))
            mv(A("MK"), IN(A("IOTA"), b16))
            mm(C("P5", 256, 496), A("I4"), A("MR"), True)
            mm(C("P5", 256, 496), A("I32"), A("MK"), False)
            act(A("BV"), C("P5", 256, 496), bias=-4096.0)
        for r in range(17):
            tt(C("EQ", 240 * r, 240 * r + 240), C("P7", 0, 240), A("LBT", S_[:, :, r:r + 16]) if r < 16 else A("BR"), eq)
            mm(PK, A("IBIG"), C("EQ", 240 * r, 240 * r + 240), False)
        scan(C("SC", 0, 240), A("RST"), PK, add, mn)
        tt(C("SM", 96, 111), C("SC", 15, 240, 16), C("SM", 80, 95), mx)
        tt(C("WI", 0, 15), C("SM", 96, 111), C("SM", 64, 79), mn)
        ts(C("WI", 16, 31), C("WI", 0, 15), 2047, band)
        w16 = C("W16", 0, 15)
        if t < 2:
            ts(C("SM", 112, 127), C("WI", 0, 15), 250 * K_, ge, 4096.0, mul)
        cp(w16, C("WI", 16, 31))
        if t < 2:
            ts(C("SM", 128, 143), C("WI", 16, 31), 1008.0, ge, 4096.0, mul)
            tt(C("SM", 144, 159), C("WI", 16, 31), C("SM", 112, 127), add)
            hn = C("P1", 0, 240)
            mm(hn, A("IB"), A("HB"), True)
            mm(hn, A("NI"), A("YO"), False)
            act(A("YW"), IN(Yw, w16))
            mm(hn, A("IB"), A("YW"), False)
            act(A("AC"), hn, AF.Abs, bias=-1.0 / 64)
            if t == 0:
                mv(A("HN"), hn)
            tt(C("SM", 160, 175), C("SM", 144, 159), C("SM", 128, 143), mx)
            tt(C("SM", 192, 207), C("SM", 160, 175), C("DUM", 0, 15), mn)
            wd16 = C("WD16", 0, 15)
            cp(wd16, C("SM", 192, 207))
            act(A("WF"), IN(A("IOTA"), w16))
            mm(C("P2", 0, 240), A("IN4"), A("NKB"), True)
            mm(C("P2", 0, 240), A("I32"), A("WF"), False)
            act(A("NEW"), C("P2", 0, 240))
            cp(A("WR"), IN(A("IOTA"), wd16))
            act(A("AF"), IN(A("AL"), wd16))
            mm(C("P3", 0, 240), A("IN4"), A("MR"), True)
            mm(C("P3", 0, 240), A("I32"), A("AF"), False)
            act(A("AG"), C("P3", 0, 240))
            for c in range(15):
                ts(A("E3", S_[:, c, 0:240 - 16 * c]), C("WR", 16 * c, 240), C("SM", 192 + c), eq, C("PC", 20), mul)
            mm(C("P6", 0, 240), A("IB"), A("THR"), True)
            mm(C("P6", 0, 240), A("OB"), A("E3", S_[:, :, 0:16]), False)
            for c in range(14):
                mm(C("P6", 16 * c + 16, 240), A("OBIG"), A("E3", S_[:, c, 16:240 - 16 * c]), False, c == 13)
            ts(A("NG"), A("AC"), 2.0, mn, 2.0, sub)
            tt(IN(A("TT"), bs16), A("NG"), A("YB"), mul)
            scan(C("DUP", 240, 480), A("RSN"), C("P6", 0, 240), add, mx)
            tt(C("SM", 208, 223), C("DUP", 255, 480, 16), C("SM", 192, 207), mx)
            tt(C("SM", 224, 239), C("SM", 208, 223), C("DUM", 0, 15), mn)
            cp(C("WS16", 0, 15), C("SM", 224, 239))
            tt(IN(A("AL"), C("WS16", 0, 15)), A("AG"), A("BV"), mx)
            cp(A("AV16"), C("AL", t + 1, V_, 7))
            tt(IN(A("NL"), bs16), A("NEW"), A("LBM"), mx)
            send("N%d" % (t + 1))
            eps_first(t + 1)
            eps_second(t + 1)
            if t == 0:
                cp(IN(A("HH"), bs16), A("HN"))
        else:
            tt(A("NEW"), IN(A("IOTA"), w16), A("MKB"), mul)
            tt(IN(A("NL"), bs16), A("NEW"), A("LBM"), mx)
            dma("y", lambda: g.sync.dma_start(T.yn[:, 0:504], T.NL[:, 0:504]), C("NL", 0, V_)[2], [], "oyn", 16)
            dma("s", lambda: g.scalar.dma_start(T.yn[:, 504:V_], T.NL[:, 504:V_]), C("NL", 0, V_)[2], [], "oyn", 16)

    queue = {"v": g.vector, "s": g.scalar, "p": g.tensor, "g": g, "y": g.sync}
    total = {}
    for o in ops:
        if o["d"] is not None:
            total[o["d"][0]] = total.get(o["d"][0], 0) + abs(o["d"][1])
    log, pred, sent, lastsend = {}, [], {}, None
    for k, o in enumerate(ops):
        p = {}
        for regs, w in ((o["r"], False), (o["w"], True)):
            for name, lo, hi, per in regs:
                ps = SCRATCH[name][0] == "psum"
                for (k2, lo2, hi2, w2, per2) in log.get(name, []):
                    o2 = ops[k2]
                    if lo2 >= hi or lo >= hi2 or not (w or w2 or ps) or k2 == k:
                        continue
                    if (per and per2 and per[0] == per2[0] and (per[2] <= per2[1] or per2[2] <= per[1])
                            and o["d"] is None and o2["d"] is None):
                        continue
                    if ps and o["q"] == "p" and o2["q"] == "p" and not o["st"] and not o2["st"] and o["g"] == o2["g"]:
                        continue
                    if o["d"] is not None and o2["d"] is not None and o["d"][0] == o2["d"][0]:
                        continue
                    p[k2] = p.get(k2, False) or w or w2
        for regs, w in ((o["r"], False), (o["w"], True)):
            for name, lo, hi, per in regs:
                h_ = log.setdefault(name, [])
                if w and o["d"] is None and o.get("st", True) and not per:
                    h_[:] = [e for e in h_ if e[1] < lo or e[2] > hi]
                h_.append((k, lo, hi, w, per))
        if "sent" in o:
            sent[o["sent"]] = k
            if lastsend is not None:
                p.setdefault(lastsend, None)
            lastsend = k
        pred.append(p)
    for k, o in enumerate(ops):
        if "comes" in o:
            pred[k][sent[o["comes"]]] = None
    succ = [[] for _ in ops]
    left = [len(p) for p in pred]
    for k, p in enumerate(pred):
        for k2 in p:
            succ[k2].append(k)
    topo_, cnt_ = [k for k in range(len(ops)) if not left[k]], list(left)
    for k in topo_:
        for k2 in succ[k]:
            cnt_[k2] -= 1
            if not cnt_[k2]:
                topo_.append(k2)
    far = [0.0] * len(ops)
    tail, rest = [0.0] * len(ops), {}
    for k in reversed(range(len(ops))):
        if ops[k]["q"] == "p" and not ops[k]["st"]:
            tail[k] = rest.get(ops[k]["g"], 0.0)
            rest[ops[k]["g"]] = tail[k] + ops[k]["c"]
    for k in reversed(topo_):
        far[k] = ops[k]["c"] + tail[k] + ops[k].get("b", 0.0) + max([far[k2] + (0 if pred[k2][k] is None else ops[k]["l"] + WAKE) for k2 in succ[k]] + [ops[k]["l"]])

    def sweep(key, before, after, forward):
        num = len(ops)
        t_, q_, c_ = [0.0] * num, [None] * num, [0.0] * num
        busy = {q: [] for q in queue}
        wait = [len(x) for x in before]
        ready = sorted((key[k], k) for k in range(num) if not wait[k])
        while ready:
            k = ready.pop(0)[1]
            pick = None
            for o in [ops[k]] + ([ops[k]["or"]] if "or" in ops[k] else []):
                q, c = o["q"], o["c"]
                t0 = 0.0 if forward else ops[k]["l"]
                for k2 in before[k]:
                    a, v = (k2, pred[k][k2]) if forward else (k, pred[k2][k])
                    free = v is None or (q_[k2] == q and (not v or q == "p" and ops[a]["d"] is None))
                    t0 = max(t0, t_[k2] + c_[k2] + (0 if free else ops[a]["l"] + WAKE))
                at_ = 0
                if q is not None:
                    iv = busy[q]
                    lo, hi = 0, len(iv)
                    while lo < hi:
                        mid = (lo + hi) // 2
                        if iv[mid][1] <= t0:
                            lo = mid + 1
                        else:
                            hi = mid
                    while lo < len(iv) and iv[lo][0] < t0 + c:
                        t0 = max(t0, iv[lo][1])
                        lo += 1
                    at_ = lo
                if pick is None or t0 + c < pick[0] + pick[2]:
                    pick = (t0, q, c, at_)
            t_[k], q_[k], c_[k] = pick[:3]
            if pick[1] is not None:
                busy[pick[1]].insert(pick[3], (pick[0], pick[0] + pick[2]))
            new = []
            for k2 in after[k]:
                wait[k2] -= 1
                if not wait[k2]:
                    new.append((key[k2], k2))
            if new:
                ready = sorted(ready + new)
        return t_, q_, c_

    if not PLAN:
        best, key = None, [o["k"] for o in ops]
        for turn in range(TURNS):
            fw = sweep(key, pred, succ, True)
            end = max(fw[0][k] + fw[2][k] + ops[k]["l"] for k in range(len(ops)))
            if best is None or end < best[0]:
                best = (end, fw)
            fw, seed, key = best[1], 12345 + turn, []
            for k in range(len(ops)):
                seed = (seed * 1103515245 + 12345) % 2147483648
                key.append(-(fw[0][k] + fw[2][k]) + (seed / 2147483648.0 * SHAKE * (1 + turn % 3) if turn > 1 else 0.0))
            bw = sweep(key, succ, pred, False)
            key = [-(bw[0][k] + bw[2][k]) for k in range(len(ops))]
        PLAN.append(best[1])
    begin, where_ = PLAN[0][0], PLAN[0][1]
    for k, o in enumerate(ops):
        if where_[k] != o["q"]:
            o.update(o["or"])
    order = sorted(range(len(ops)), key=lambda k: (begin[k], k))
    place = {k: i for i, k in enumerate(order)}
    closes = {}
    for k in order:
        if ops[k]["q"] == "p":
            closes[ops[k]["g"]] = k
    seen, deps, marked = {}, {}, set()
    for k in order:
        q, need = ops[k]["q"], {}
        for k2, v in pred[k].items():
            o2 = ops[k2]
            if v is None or (o2["q"] == q and (not v or q == "p" and o2["d"] is None)):
                continue
            kq = o2["d"][0] if o2["d"] is not None else "e" + o2["q"]
            if kq not in need or place[k2] > place[need[kq]]:
                need[kq] = k2
        for kq in list(need):
            val = place[need[kq]] if ops[need[kq]]["d"] is None else 0
            if seen.get((q, kq), -1) >= val:
                del need[kq]
            else:
                seen[(q, kq)] = val
                if ops[need[kq]]["d"] is None:
                    marked.add(need[kq])
        deps[k] = need
    count, at = {}, {}
    for k in order:
        q, fn, ds = ops[k]["q"], ops[k]["f"], ops[k]["d"]
        if q is None:
            continue
        for kq, k2 in deps[k].items():
            queue[q].wait_ge(T.sem[kq], at[k2] if ops[k2]["d"] is None else total[kq])
        ins = fn(closes[ops[k]["g"]] == k) if q == "p" else fn()
        if ds is not None:
            if ds[1] > 0:
                ins.then_inc(T.sem[ds[0]], ds[1])
        elif k in marked:
            count[q] = count.get(q, 0) + 1
            at[k] = count[q]
            ins.then_inc(T.sem["e" + q], 1)
    for q, c in count.items():
        g.wait_ge(T.sem["e" + q], c)
    for s, c in total.items():
        g.wait_ge(T.sem[s], c)
